import numpy as np
CORES = [1,5,73,77,129,133,201,205]
N = 8
DEAD = {"mate_links":[[1,0],[1,1]],"switch_ports":[],"chips":[1]}
def setup_inputs(rng):
    return {"x": rng.standard_normal((N, 128, 128), dtype=np.float32)}
def reference(x):
    s = x.sum(axis=0, dtype=np.float64).astype(x.dtype)
    return {"y": np.broadcast_to(s, (N,) + s.shape)}

@@ -1,0 +1,146 @@
+from concourse.bass import DstId, RemoteDMATransfer
+from concourse.mybir import AluOpType
+
+ROWS, COLS = 128, 128
+SLICES = 4
+W = ROWS * COLS // (SLICES * 128)
+PLANE_RANKS = 4
+
+SCRATCH = {
+    "xs": ("dram", [SLICES, 128, W], "float32"),
+    "part": ("dram", [PLANE_RANKS, 128, W], "float32"),
+    "mine": ("dram", [SLICES, 128, W], "float32"),
+    "theirs": ("dram", [SLICES, 128, W], "float32"),
+}
+SEMAPHORES = ["loaded", "sent", "got", "got_mine", "got_theirs", "stored", "done"]
+
+
+def _bits(mask):
+    return [1 << i for i in range(mask.bit_length()) if (mask >> i) & 1]
+
+
+def _deal(bits, parts):
+    per = 1
+    while per * 2 * parts <= len(bits):
+        per *= 2
+    return [sum(bits[i * per:(i + 1) * per]) for i in range(parts)]
+
+
+def _count(mask):
+    return len(_bits(mask))
+
+
+def _plan(T, topo):
+    ranks = list(T.cores)
+    dead = T.tables["DEAD"]
+    world = range((max(topo.host(c) for c in ranks) + 1) * topo.CORES_PER_HOST)
+
+    def gid(c):
+        return topo.CHIPS * topo.host(c) + topo.chip(c)
+
+    no_chip = set(dead["chips"])
+    no_mate = set((c, d) for c, d in dead["mate_links"])
+    no_port = set((c, d) for c, d in dead["switch_ports"])
+
+    def way_ok(src, dst):
+        if gid(src) in no_chip or gid(dst) in no_chip or not topo.may_write(src, dst):
+            return False
+        if gid(src) == gid(dst):
+            return True
+        d, at = topo.die(src), gid(src)
+        if not topo.same_plane(src, dst):
+            mate = gid([c for c in world if topo.mates(src, c)][0])
+            if mate in no_chip or (at, d) in no_mate or (mate, d) in no_mate:
+                return False
+            at = mate
+        if at == gid(dst):
+            return True
+        return (at, d) not in no_port and (gid(dst), d) not in no_port
+
+    chips = []
+    for r in ranks:
+        if gid(r) not in chips:
+            chips.append(gid(r))
+    on = {x: [r for r in ranks if gid(r) == x] for x in chips}
+    plane = {x: [z for z in chips if z == x or topo.same_plane(on[x][0], on[z][0])] for x in chips}
+
+    helpers = {}
+    for x in chips:
+        across = [r for r in ranks if gid(r) not in plane[x]]
+        own = [c for c in world if gid(c) == x and c not in ranks and all(topo.may_write(c, r) for r in across)]
+        helpers[x] = own[:SLICES]
+
+    gate, load = {}, {x: 0 for x in chips}
+    order = sorted(chips, key=lambda x: len([z for z in chips if z not in plane[x]
+                                             and all(way_ok(h, r) for h in helpers[z] for r in on[x])]))
+    for x in order:
+        can = [z for z in chips if z not in plane[x] and all(way_ok(h, r) for h in helpers[z] for r in on[x])]
+        gate[x] = min(can, key=lambda z: (load[z], topo.host(on[z][0]) != topo.host(on[x][0])))
+        load[gate[x]] += 1
+
+    def scatter(r):
+        x = gid(r)
+        slot = [q for z in plane[x] for q in on[z]].index(r)
+        far = [(h, s) for z in plane[x] if z != x for s, h in enumerate(helpers[z])]
+        near = [(h, s) for s, h in enumerate(helpers[x])]
+        out = _bits(min(topo.mask(r, h) for h, _ in far))
+        stay = [b for b in _bits(topo.mask(r, near[0][0])) if b not in out]
+        return ([(h, s, slot, m) for (h, s), m in zip(near, _deal(stay, len(near)))]
+                + [(h, s, slot, m) for (h, s), m in zip(far, _deal(out, len(far)))])
+
+    def fold(h):
+        x = gid(h)
+        near = on[x]
+        far = [r for z in chips if gate[z] == x for r in on[z]]
+        stay = _bits(topo.mask(h, near[0]))
+        res = []
+        if far:
+            out = _bits(min(topo.mask(h, r) for r in far))
+            stay = [b for b in stay if b not in out]
+            res += [(r, "theirs", m) for r, m in zip(far, _deal(out, len(far)))]
+        return res + [(r, "mine", m) for r, m in zip(near, _deal(stay, len(near)))]
+
+    piece = {h: s for x in chips for s, h in enumerate(helpers[x])}
+    return ranks, piece, scatter, fold
+
+
+def rank_program(g, core, T, topo):
+    ranks, piece, scatter, fold = _plan(T, topo)
+
+    def dst(c):
+        rid, pid = topo.addr(c, core)
+        return DstId(rid=rid, pnc=pid)
+
+    if core in piece:
+        s = piece[core]
+        g.wait_ge(T.sem.got, sum(_count(m) for r in ranks for h, _, _, m in scatter(r) if h == core))
+        todo = fold(core)
+        g.remote_dma_fused(
+            [RemoteDMATransfer(dst_ids=[dst(r)], dma_engine_mask=m, remote_sem=T.sem["got_" + buf],
+                               srcs=[T.part[i] for i in range(PLANE_RANKS)], dsts=[T[buf][s]], alu_op=1)
+             for r, buf, m in todo],
+            local_sem=T.sem.sent)
+        g.wait_ge(T.sem.sent, sum(_count(m) for _, _, m in todo))
+        return
+
+    if core not in ranks:
+        return
+
+    g.sync.dma_start(T.xs[:], T.x[:]).then_inc(T.sem.loaded, 16)
+    g.wait_ge(T.sem.loaded, 16)
+    todo = scatter(core)
+    g.remote_dma_fused(
+        [RemoteDMATransfer(dst_ids=[dst(h)], dma_engine_mask=m, remote_sem=T.sem.got, src=T.xs[s], dst=T.part[slot])
+         for h, s, slot, m in todo],
+        local_sem=T.sem.sent)
+
+    need = {buf: sum(_count(m) for h in piece for r, b, m in fold(h) if r == core and b == buf)
+            for buf in ("mine", "theirs")}
+    g.sync.wait_ge(T.sem.got_mine, need["mine"])
+    g.sync.dma_start(T.y[:], T.mine[:]).then_inc(T.sem.stored, 16)
+
+    g.wait_ge(T.sem.sent, sum(_count(m) for _, _, _, m in todo))
+    g.wait_ge(T.sem.got_theirs, need["theirs"])
+    g.wait_ge(T.sem.stored, 16)
+    g.dma_start(T.y[:], T.theirs[:], accum_op=AluOpType.add, max_dma_last_dim=4096).then_inc(T.sem.done, 16)
+    g.wait_ge(T.sem.done, 16)

@@ -1,5 +1,4 @@
 from concourse.bass import DstId, RemoteDMATransfer
-from concourse.mybir import AluOpType
 
 ROWS, COLS = 128, 128
 SLICES = 4
@@ -8,11 +7,10 @@ PLANE_RANKS = 4
 
 SCRATCH = {
     "xs": ("dram", [SLICES, 128, W], "float32"),
-    "part": ("dram", [PLANE_RANKS, 128, W], "float32"),
-    "mine": ("dram", [SLICES, 128, W], "float32"),
-    "theirs": ("dram", [SLICES, 128, W], "float32"),
+    "part": ("dram", [PLANE_RANKS + 1, 128, W], "float32"),
+    "res": ("dram", [SLICES, 128, W], "float32"),
 }
-SEMAPHORES = ["loaded", "sent", "got", "got_mine", "got_theirs", "stored", "done"]
+SEMAPHORES = ["loaded", "sent", "got", "got_other", "got_res", "stored"]
 
 
 def _bits(mask):
@@ -70,13 +68,16 @@ def _plan(T, topo):
         own = [c for c in world if gid(c) == x and c not in ranks and all(topo.may_write(c, r) for r in across)]
         helpers[x] = own[:SLICES]
 
+    def serves(z, x):
+        return z not in plane[x] and all(way_ok(a, b) for a, b in zip(helpers[z], helpers[x]))
+
     gate, load = {}, {x: 0 for x in chips}
-    order = sorted(chips, key=lambda x: len([z for z in chips if z not in plane[x]
-                                             and all(way_ok(h, r) for h in helpers[z] for r in on[x])]))
-    for x in order:
-        can = [z for z in chips if z not in plane[x] and all(way_ok(h, r) for h in helpers[z] for r in on[x])]
+    for x in sorted(chips, key=lambda x: len([z for z in chips if serves(z, x)])):
+        can = [z for z in chips if serves(z, x)]
         gate[x] = min(can, key=lambda z: (load[z], topo.host(on[z][0]) != topo.host(on[x][0])))
         load[gate[x]] += 1
+
+    piece = {h: s for x in chips for s, h in enumerate(helpers[x])}
 
     def scatter(r):
         x = gid(r)
@@ -88,24 +89,21 @@ def _plan(T, topo):
         return ([(h, s, slot, m) for (h, s), m in zip(near, _deal(stay, len(near)))]
                 + [(h, s, slot, m) for (h, s), m in zip(far, _deal(out, len(far)))])
 
-    def fold(h):
-        x = gid(h)
-        near = on[x]
-        far = [r for z in chips if gate[z] == x for r in on[z]]
-        stay = _bits(topo.mask(h, near[0]))
-        res = []
-        if far:
-            out = _bits(min(topo.mask(h, r) for r in far))
-            stay = [b for b in stay if b not in out]
-            res += [(r, "theirs", m) for r, m in zip(far, _deal(out, len(far)))]
-        return res + [(r, "mine", m) for r, m in zip(near, _deal(stay, len(near)))]
+    def cross(h):
+        far = [helpers[z][piece[h]] for z in chips if gate[z] == gid(h)]
+        if not far:
+            return []
+        return list(zip(far, _deal(_bits(min(topo.mask(h, f) for f in far)), len(far))))
 
-    piece = {h: s for x in chips for s, h in enumerate(helpers[x])}
-    return ranks, piece, scatter, fold
+    def finish(h):
+        near = on[gid(h)]
+        return list(zip(near, _deal(_bits(min(topo.mask(h, r) for r in near)), len(near))))
+
+    return ranks, piece, scatter, cross, finish
 
 
 def rank_program(g, core, T, topo):
-    ranks, piece, scatter, fold = _plan(T, topo)
+    ranks, piece, scatter, cross, finish = _plan(T, topo)
 
     def dst(c):
         rid, pid = topo.addr(c, core)
@@ -113,14 +111,25 @@ def rank_program(g, core, T, topo):
 
     if core in piece:
         s = piece[core]
+        sent = 0
         g.wait_ge(T.sem.got, sum(_count(m) for r in ranks for h, _, _, m in scatter(r) if h == core))
-        todo = fold(core)
+        todo = cross(core)
+        if todo:
+            g.remote_dma_fused(
+                [RemoteDMATransfer(dst_ids=[dst(h)], dma_engine_mask=m, remote_sem=T.sem.got_other,
+                                   srcs=[T.part[i] for i in range(PLANE_RANKS)], dsts=[T.part[PLANE_RANKS]], alu_op=1)
+                 for h, m in todo],
+                local_sem=T.sem.sent)
+            sent += sum(_count(m) for _, m in todo)
+        g.wait_ge(T.sem.got_other, sum(_count(m) for a in piece for h, m in cross(a) if h == core))
+        todo = finish(core)
         g.remote_dma_fused(
-            [RemoteDMATransfer(dst_ids=[dst(r)], dma_engine_mask=m, remote_sem=T.sem["got_" + buf],
-                               srcs=[T.part[i] for i in range(PLANE_RANKS)], dsts=[T[buf][s]], alu_op=1)
-             for r, buf, m in todo],
+            [RemoteDMATransfer(dst_ids=[dst(r)], dma_engine_mask=m, remote_sem=T.sem.got_res,
+                               srcs=[T.part[i] for i in range(PLANE_RANKS + 1)], dsts=[T.res[s]], alu_op=1)
+             for r, m in todo],
             local_sem=T.sem.sent)
-        g.wait_ge(T.sem.sent, sum(_count(m) for _, _, m in todo))
+        sent += sum(_count(m) for _, m in todo)
+        g.wait_ge(T.sem.sent, sent)
         return
 
     if core not in ranks:
@@ -134,13 +143,8 @@ def rank_program(g, core, T, topo):
          for h, s, slot, m in todo],
         local_sem=T.sem.sent)
 
-    need = {buf: sum(_count(m) for h in piece for r, b, m in fold(h) if r == core and b == buf)
-            for buf in ("mine", "theirs")}
-    g.sync.wait_ge(T.sem.got_mine, need["mine"])
-    g.sync.dma_start(T.y[:], T.mine[:]).then_inc(T.sem.stored, 16)
+    g.sync.wait_ge(T.sem.got_res, sum(_count(m) for h in piece for r, m in finish(h) if r == core))
+    g.sync.dma_start(T.y[:], T.res[:]).then_inc(T.sem.stored, 16)
 
     g.wait_ge(T.sem.sent, sum(_count(m) for _, _, _, m in todo))
-    g.wait_ge(T.sem.got_theirs, need["theirs"])
     g.wait_ge(T.sem.stored, 16)
-    g.dma_start(T.y[:], T.theirs[:], accum_op=AluOpType.add, max_dma_last_dim=4096).then_inc(T.sem.done, 16)
-    g.wait_ge(T.sem.done, 16)

@@ -86,8 +86,8 @@ def _plan(T, topo):
         near = [(h, s) for s, h in enumerate(helpers[x])]
         out = _bits(min(topo.mask(r, h) for h, _ in far))
         stay = [b for b in _bits(topo.mask(r, near[0][0])) if b not in out]
-        return ([(h, s, slot, m) for (h, s), m in zip(near, _deal(stay, len(near)))]
-                + [(h, s, slot, m) for (h, s), m in zip(far, _deal(out, len(far)))])
+        return ([(h, s, slot, m) for (h, s), m in zip(far, _deal(out, len(far)))]
+                + [(h, s, slot, m) for (h, s), m in zip(near, _deal(stay, len(near)))])
 
     def cross(h):
         far = [helpers[z][piece[h]] for z in chips if gate[z] == gid(h)]

@@ -4,13 +4,15 @@ ROWS, COLS = 128, 128
 SLICES = 4
 W = ROWS * COLS // (SLICES * 128)
 PLANE_RANKS = 4
+STORES = 2
 
 SCRATCH = {
     "xs": ("dram", [SLICES, 128, W], "float32"),
     "part": ("dram", [PLANE_RANKS + 1, 128, W], "float32"),
     "res": ("dram", [SLICES, 128, W], "float32"),
 }
-SEMAPHORES = ["loaded", "sent", "got", "got_other", "got_res", "stored"]
+SEMAPHORES = (["loaded", "sent", "got", "got_other"]
+              + ["got_res%d" % k for k in range(STORES)] + ["stored%d" % k for k in range(STORES)])
 
 
 def _bits(mask):
@@ -69,13 +71,9 @@ def _plan(T, topo):
         helpers[x] = own[:SLICES]
 
     def serves(z, x):
-        return z not in plane[x] and all(way_ok(a, b) for a, b in zip(helpers[z], helpers[x]))
+        return all(way_ok(a, b) for a, b in zip(helpers[z], helpers[x]))
 
-    gate, load = {}, {x: 0 for x in chips}
-    for x in sorted(chips, key=lambda x: len([z for z in chips if serves(z, x)])):
-        can = [z for z in chips if serves(z, x)]
-        gate[x] = min(can, key=lambda z: (load[z], topo.host(on[z][0]) != topo.host(on[x][0])))
-        load[gate[x]] += 1
+    gateway = {x: [z for z in plane[x] if all(serves(z, o) for o in chips if o not in plane[x])][-1] for x in chips}
 
     piece = {h: s for x in chips for s, h in enumerate(helpers[x])}
 
@@ -86,13 +84,15 @@ def _plan(T, topo):
         near = [(h, s) for s, h in enumerate(helpers[x])]
         out = _bits(min(topo.mask(r, h) for h, _ in far))
         stay = [b for b in _bits(topo.mask(r, near[0][0])) if b not in out]
-        return ([(h, s, slot, m) for (h, s), m in zip(far, _deal(out, len(far)))]
+        todo = ([(h, s, slot, m) for (h, s), m in zip(far, _deal(out, len(far)))]
                 + [(h, s, slot, m) for (h, s), m in zip(near, _deal(stay, len(near)))])
+        return sorted(todo, key=lambda t: gid(t[0]) != gateway[x])
 
     def cross(h):
-        far = [helpers[z][piece[h]] for z in chips if gate[z] == gid(h)]
-        if not far:
+        x = gid(h)
+        if gateway[x] != x:
             return []
+        far = [helpers[z][piece[h]] for z in chips if z not in plane[x]]
         return list(zip(far, _deal(_bits(min(topo.mask(h, f) for f in far)), len(far))))
 
     def finish(h):
@@ -104,6 +104,7 @@ def _plan(T, topo):
 
 def rank_program(g, core, T, topo):
     ranks, piece, scatter, cross, finish = _plan(T, topo)
+    per = SLICES // STORES
 
     def dst(c):
         rid, pid = topo.addr(c, core)
@@ -124,7 +125,7 @@ def rank_program(g, core, T, topo):
         g.wait_ge(T.sem.got_other, sum(_count(m) for a in piece for h, m in cross(a) if h == core))
         todo = finish(core)
         g.remote_dma_fused(
-            [RemoteDMATransfer(dst_ids=[dst(r)], dma_engine_mask=m, remote_sem=T.sem.got_res,
+            [RemoteDMATransfer(dst_ids=[dst(r)], dma_engine_mask=m, remote_sem=T.sem["got_res%d" % (s // per)],
                                srcs=[T.part[i] for i in range(PLANE_RANKS + 1)], dsts=[T.res[s]], alu_op=1)
              for r, m in todo],
             local_sem=T.sem.sent)
@@ -143,8 +144,12 @@ def rank_program(g, core, T, topo):
          for h, s, slot, m in todo],
         local_sem=T.sem.sent)
 
-    g.sync.wait_ge(T.sem.got_res, sum(_count(m) for h in piece for r, m in finish(h) if r == core))
-    g.sync.dma_start(T.y[:], T.res[:]).then_inc(T.sem.stored, 16)
+    rows = ROWS // STORES
+    for k, q in enumerate([g.sync, g.scalar][:STORES]):
+        q.wait_ge(T.sem["got_res%d" % k],
+                  sum(_count(m) for h in piece for r, m in finish(h) if r == core and piece[h] // per == k))
+        q.dma_start(T.y[k * rows:(k + 1) * rows, :], T.res[k * per:(k + 1) * per]).then_inc(T.sem["stored%d" % k], 16)
 
     g.wait_ge(T.sem.sent, sum(_count(m) for _, _, _, m in todo))
-    g.wait_ge(T.sem.stored, 16)
+    for k in range(STORES):
+        g.wait_ge(T.sem["stored%d" % k], 16)

@@ -91,13 +91,13 @@ def _plan(T, topo):
     def cross(h):
         x = gid(h)
         if gateway[x] != x:
-            return []
+            return [], 0
         far = [helpers[z][piece[h]] for z in chips if z not in plane[x]]
-        return list(zip(far, _deal(_bits(min(topo.mask(h, f) for f in far)), len(far))))
+        return far, min(topo.mask(h, f) for f in far)
 
     def finish(h):
         near = on[gid(h)]
-        return list(zip(near, _deal(_bits(min(topo.mask(h, r) for r in near)), len(near))))
+        return near, min(topo.mask(h, r) for r in near)
 
     return ranks, piece, scatter, cross, finish
 
@@ -110,26 +110,29 @@ def rank_program(g, core, T, topo):
         rid, pid = topo.addr(c, core)
         return DstId(rid=rid, pnc=pid)
 
+    def lands(hop, who, keep):
+        return sum(_count(hop(a)[1]) for a in piece if who in hop(a)[0] and keep(a))
+
     if core in piece:
         s = piece[core]
         sent = 0
         g.wait_ge(T.sem.got, sum(_count(m) for r in ranks for h, _, _, m in scatter(r) if h == core))
-        todo = cross(core)
-        if todo:
+        to, m = cross(core)
+        if to:
             g.remote_dma_fused(
-                [RemoteDMATransfer(dst_ids=[dst(h)], dma_engine_mask=m, remote_sem=T.sem.got_other,
-                                   srcs=[T.part[i] for i in range(PLANE_RANKS)], dsts=[T.part[PLANE_RANKS]], alu_op=1)
-                 for h, m in todo],
+                [RemoteDMATransfer(dst_ids=[dst(h) for h in to], dma_engine_mask=m, remote_sem=T.sem.got_other,
+                                   srcs=[T.part[i] for i in range(PLANE_RANKS)],
+                                   dsts=[T.part[PLANE_RANKS] for _ in to], alu_op=1)],
                 local_sem=T.sem.sent)
-            sent += sum(_count(m) for _, m in todo)
-        g.wait_ge(T.sem.got_other, sum(_count(m) for a in piece for h, m in cross(a) if h == core))
-        todo = finish(core)
+            sent += _count(m)
+        g.wait_ge(T.sem.got_other, lands(cross, core, lambda a: True))
+        to, m = finish(core)
         g.remote_dma_fused(
-            [RemoteDMATransfer(dst_ids=[dst(r)], dma_engine_mask=m, remote_sem=T.sem["got_res%d" % (s // per)],
-                               srcs=[T.part[i] for i in range(PLANE_RANKS + 1)], dsts=[T.res[s]], alu_op=1)
-             for r, m in todo],
+            [RemoteDMATransfer(dst_ids=[dst(r) for r in to], dma_engine_mask=m, remote_sem=T.sem["got_res%d" % (s // per)],
+                               srcs=[T.part[i] for i in range(PLANE_RANKS + 1)],
+                               dsts=[T.res[s] for _ in to], alu_op=1)],
             local_sem=T.sem.sent)
-        sent += sum(_count(m) for _, m in todo)
+        sent += _count(m)
         g.wait_ge(T.sem.sent, sent)
         return
 
@@ -146,8 +149,7 @@ def rank_program(g, core, T, topo):
 
     rows = ROWS // STORES
     for k, q in enumerate([g.sync, g.scalar][:STORES]):
-        q.wait_ge(T.sem["got_res%d" % k],
-                  sum(_count(m) for h in piece for r, m in finish(h) if r == core and piece[h] // per == k))
+        q.wait_ge(T.sem["got_res%d" % k], lands(finish, core, lambda a: piece[a] // per == k))
         q.dma_start(T.y[k * rows:(k + 1) * rows, :], T.res[k * per:(k + 1) * per]).then_inc(T.sem["stored%d" % k], 16)
 
     g.wait_ge(T.sem.sent, sum(_count(m) for _, _, _, m in todo))

from concourse.bass import DstId, RemoteDMATransfer

ROWS, COLS = 128, 128
SLICES = 4
W = ROWS * COLS // (SLICES * 128)
PLANE_RANKS = 4
STORES = 2

SCRATCH = {
    "xs": ("dram", [SLICES, 128, W], "float32"),
    "part": ("dram", [PLANE_RANKS + 1, 128, W], "float32"),
    "res": ("dram", [SLICES, 128, W], "float32"),
}
SEMAPHORES = (["loaded", "sent", "got", "got_other"]
              + ["got_res%d" % k for k in range(STORES)] + ["stored%d" % k for k in range(STORES)])


def _bits(mask):
    return [1 << i for i in range(mask.bit_length()) if (mask >> i) & 1]


def _deal(bits, parts):
    per = 1
    while per * 2 * parts <= len(bits):
        per *= 2
    return [sum(bits[i * per:(i + 1) * per]) for i in range(parts)]


def _count(mask):
    return len(_bits(mask))


def _plan(T, topo):
    ranks = list(T.cores)
    dead = T.tables["DEAD"]
    world = range((max(topo.host(c) for c in ranks) + 1) * topo.CORES_PER_HOST)

    def gid(c):
        return topo.CHIPS * topo.host(c) + topo.chip(c)

    no_chip = set(dead["chips"])
    no_mate = set((c, d) for c, d in dead["mate_links"])
    no_port = set((c, d) for c, d in dead["switch_ports"])

    def way_ok(src, dst):
        if gid(src) in no_chip or gid(dst) in no_chip or not topo.may_write(src, dst):
            return False
        if gid(src) == gid(dst):
            return True
        d, at = topo.die(src), gid(src)
        if not topo.same_plane(src, dst):
            mate = gid([c for c in world if topo.mates(src, c)][0])
            if mate in no_chip or (at, d) in no_mate or (mate, d) in no_mate:
                return False
            at = mate
        if at == gid(dst):
            return True
        return (at, d) not in no_port and (gid(dst), d) not in no_port

    chips = []
    for r in ranks:
        if gid(r) not in chips:
            chips.append(gid(r))
    on = {x: [r for r in ranks if gid(r) == x] for x in chips}
    plane = {x: [z for z in chips if z == x or topo.same_plane(on[x][0], on[z][0])] for x in chips}

    helpers = {}
    for x in chips:
        across = [r for r in ranks if gid(r) not in plane[x]]
        own = [c for c in world if gid(c) == x and c not in ranks and all(topo.may_write(c, r) for r in across)]
        helpers[x] = own[:SLICES]

    def serves(z, x):
        return all(way_ok(a, b) for a, b in zip(helpers[z], helpers[x]))

    gateway = {x: [z for z in plane[x] if all(serves(z, o) for o in chips if o not in plane[x])][-1] for x in chips}

    piece = {h: s for x in chips for s, h in enumerate(helpers[x])}

    def scatter(r):
        x = gid(r)
        slot = [q for z in plane[x] for q in on[z]].index(r)
        far = [(h, s) for z in plane[x] if z != x for s, h in enumerate(helpers[z])]
        near = [(h, s) for s, h in enumerate(helpers[x])]
        out = _bits(min(topo.mask(r, h) for h, _ in far))
        stay = [b for b in _bits(topo.mask(r, near[0][0])) if b not in out]
        todo = ([(h, s, slot, m) for (h, s), m in zip(far, _deal(out, len(far)))]
                + [(h, s, slot, m) for (h, s), m in zip(near, _deal(stay, len(near)))])
        return sorted(todo, key=lambda t: gid(t[0]) != gateway[x])

    def cross(h):
        x = gid(h)
        if gateway[x] != x:
            return [], 0
        far = [helpers[z][piece[h]] for z in chips if z not in plane[x]]
        return far, min(topo.mask(h, f) for f in far)

    def finish(h):
        near = on[gid(h)]
        return near, min(topo.mask(h, r) for r in near)

    return ranks, piece, scatter, cross, finish


def rank_program(g, core, T, topo):
    ranks, piece, scatter, cross, finish = _plan(T, topo)
    per = SLICES // STORES

    def dst(c):
        rid, pid = topo.addr(c, core)
        return DstId(rid=rid, pnc=pid)

    def lands(hop, who, keep):
        return sum(_count(hop(a)[1]) for a in piece if who in hop(a)[0] and keep(a))

    if core in piece:
        s = piece[core]
        sent = 0
        g.wait_ge(T.sem.got, sum(_count(m) for r in ranks for h, _, _, m in scatter(r) if h == core))
        to, m = cross(core)
        if to:
            g.remote_dma_fused(
                [RemoteDMATransfer(dst_ids=[dst(h) for h in to], dma_engine_mask=m, remote_sem=T.sem.got_other,
                                   srcs=[T.part[i] for i in range(PLANE_RANKS)],
                                   dsts=[T.part[PLANE_RANKS] for _ in to], alu_op=1)],
                local_sem=T.sem.sent)
            sent += _count(m)
        g.wait_ge(T.sem.got_other, lands(cross, core, lambda a: True))
        to, m = finish(core)
        g.remote_dma_fused(
            [RemoteDMATransfer(dst_ids=[dst(r) for r in to], dma_engine_mask=m, remote_sem=T.sem["got_res%d" % (s // per)],
                               srcs=[T.part[i] for i in range(PLANE_RANKS + 1)],
                               dsts=[T.res[s] for _ in to], alu_op=1)],
            local_sem=T.sem.sent)
        sent += _count(m)
        g.wait_ge(T.sem.sent, sent)
        return

    if core not in ranks:
        return

    g.sync.dma_start(T.xs[:], T.x[:]).then_inc(T.sem.loaded, 16)
    g.wait_ge(T.sem.loaded, 16)
    todo = scatter(core)
    g.remote_dma_fused(
        [RemoteDMATransfer(dst_ids=[dst(h)], dma_engine_mask=m, remote_sem=T.sem.got, src=T.xs[s], dst=T.part[slot])
         for h, s, slot, m in todo],
        local_sem=T.sem.sent)

    rows = ROWS // STORES
    for k, q in enumerate([g.sync, g.scalar][:STORES]):
        q.wait_ge(T.sem["got_res%d" % k], lands(finish, core, lambda a: piece[a] // per == k))
        q.dma_start(T.y[k * rows:(k + 1) * rows, :], T.res[k * per:(k + 1) * per]).then_inc(T.sem["stored%d" % k], 16)

    g.wait_ge(T.sem.sent, sum(_count(m) for _, _, _, m in todo))
    for k in range(STORES):
        g.wait_ge(T.sem["stored%d" % k], 16)
